import numpy as np
import ml_dtypes


def mxq(x, axis, fmt="e4m3"):
    dtype, down = {"e4m3": (ml_dtypes.float8_e4m3fn, 7), "e5m2": (ml_dtypes.float8_e5m2, 14)}[fmt]
    v = np.moveaxis(np.asarray(x, np.float32).astype(ml_dtypes.bfloat16).astype(np.float64), axis, -1)
    blocks = v.reshape(v.shape[:-1] + (-1, 32))
    amax = np.abs(blocks).max(-1, keepdims=True)
    byte = np.maximum(np.where(amax > 0, np.frexp(amax)[1] - 1 + 127, 0) - down, 1)
    scale = np.exp2(byte - 127.0)
    codes = (blocks / scale).astype(np.float32).astype(dtype).astype(np.float64)
    return np.moveaxis((codes * scale).reshape(v.shape), -1, axis)


WIDE = False


def mx_kscale(k):
    if not WIDE:
        return np.ones(k)
    levels = np.array([10, -10, 5, -5, 0])
    if k % 512:
        return np.exp2(np.random.permutation(np.resize(levels, k // 32))).repeat(32)
    a = np.empty((k // 512, 16))
    for p in range(k // 512):
        a[p, :8] = np.random.permutation(np.resize(levels, 8))
        for g in range(8):
            far = levels[np.abs(levels - a[p, g]) >= 10]
            a[p, g + 8] = far[np.random.randint(len(far))]
    return np.exp2(a.ravel()).repeat(32)


def f64(x):
    return np.asarray(x).astype(np.float64)


def striped(idx):
    return np.tile(idx.reshape(-1, 16).T, (8, 1)).astype(np.uint16)


def unstriped(offs):
    return offs[:16].T.reshape(-1).astype(np.int64)


def gelu(v):
    return 0.5 * v * (1.0 + np.tanh(np.sqrt(2.0 / np.pi) * (v + 0.044715 * v**3)))


K, T, E, C, N = 1536, 768, 18, 128, 128
TOP = 3


def by_expert(wq, xq):
    return np.concatenate([wq[e].T @ xq[:, e * C:(e + 1) * C] for e in range(E)], axis=1)


def setup_inputs():
    n = np.random.standard_normal
    s = mx_kscale(K)[:, None]
    deal = np.repeat(np.arange(E), C).reshape(TOP, T)[:, np.random.permutation(T)]
    deal = np.take_along_axis(deal, np.argsort(np.random.rand(TOP, T), axis=0), axis=0)
    for _ in range(8):
        s_, t_ = np.random.permutation(T).reshape(2, -1); r = np.random.randint(TOP, size=T // 2); x, y = deal[r, s_].copy(), deal[r, t_].copy()
        ok = ~((deal[:, s_] == y).any(0) | (deal[:, t_] == x).any(0)); deal[r[ok], s_[ok]] = y[ok]; deal[r[ok], t_[ok]] = x[ok]
    order = np.lexsort((np.random.rand(TOP * T), deal.reshape(-1)))
    slot_token = order % T; pos = np.empty(TOP * T, np.int64); pos[order] = np.arange(TOP * T); pos = pos.reshape(TOP, T)
    g = np.random.uniform(0.5, 1.5, (TOP, T)); g = g / g.sum(0)
    return {
        "xT": (n((K, T)) * s).astype(np.float32),
        "w": (n((E, K, N)) / np.sqrt(K) / s[None]).astype(np.float32),
        "b": (0.3 * n((N, E))).astype(np.float32),
        "gate": np.stack([np.tile(r, (N, 1)) for r in g]).astype(np.float32),
        "offs": striped(slot_token),
        "pos1": striped(pos[0]),
        "pos2": striped(pos[1]),
        "pos3": striped(pos[2]),
    }


def reference(xT, w, b, gate, offs, pos1, pos2, pos3):
    idx = unstriped(offs)
    xq = mxq(f64(xT)[:, idx], 0, "e4m3")
    y = by_expert(mxq(f64(w), 1, "e4m3"), xq)
    y = gelu(y + np.repeat(f64(b), C, axis=1))
    return sum(f64(gate[r]) * y[:, unstriped(p)] for r, p in enumerate((pos1, pos2, pos3)))

@@ -1,0 +1,265 @@
+from contextlib import ExitStack
+
+import concourse.mybir as mybir
+
+K, T, E, C, N = 1536, 768, 18, 128, 128
+TOP = 3
+FLOPS = 2 * K * N * TOP * T
+
+F32 = mybir.dt.float32
+BF16 = mybir.dt.bfloat16
+U32 = mybir.dt.uint32
+U16 = mybir.dt.uint16
+U8 = mybir.dt.uint8
+FP8X4 = mybir.dt.float8_e4m3fn_x4
+ACT = mybir.ActivationFunctionType
+ALU = mybir.AluOpType
+
+P = 128
+PACK = 4
+K_PASS = P * PACK
+PASSES = K // K_PASS
+SLOTS = E * C
+W_PASSES = E * PASSES
+PASS_COLS = PACK * N
+
+X_CHUNKS = ((0, 0, 128), (0, 128, 128), (0, 256, 512), (1, 0, 512), (1, 512, 256), (2, 0, 512), (2, 512, 256))
+W_LOADS = [4] * 12 + [2, 2, 1, 1]
+LOADS_AHEAD = 10
+SLICES = ((0, 512), (512, 512), (1024, 512), (1536, 512), (2048, 256))
+SLICE_BUFS = 3
+VECTOR_X = (1, 6)
+BIAS_AFTER = 14
+VECTOR_W = (17, 20, 22, 25, 26, 27)
+GELU_LAG = 7
+COMBINE = ((0, 512), (512, 256))
+
+
+def tile_moe_tk_lin_gelu_kernel(tc, xT, w, b, gate, offs, pos1, pos2, pos3, out):
+    nc = tc.nc
+    with ExitStack() as ctx:
+        held = ctx.enter_context(tc.tile_pool(name="held", bufs=1))
+        stream = ctx.enter_context(tc.tile_pool(name="stream", bufs=12))
+        x_stage = ctx.enter_context(tc.tile_pool(name="x_stage", bufs=3))
+        w_stage = ctx.enter_context(tc.tile_pool(name="w_stage", bufs=6))
+        slots_pool = ctx.enter_context(tc.tile_pool(name="slots_pool", bufs=SLICE_BUFS))
+        ends = ctx.enter_context(tc.tile_pool(name="ends", bufs=1))
+        psum = ctx.enter_context(tc.psum_pool(name="psum", bufs=8))
+
+        slot_list = held.tile([P, SLOTS // 16], U16, name="slot_list")
+        place_lists = [held.tile([P, T // 16], U16, name=f"place_list{r}") for r in range(TOP)]
+        bias = held.tile([P, E], F32, name="bias")
+        x_codes = [held.tile([P, T], U32, name=f"x_codes{a}", align_bytes=64) for a in range(PASSES)]
+        x_scales = held.tile([P, T], U8, name="x_scales", align_bytes=64)
+        w_codes = held.tile([P, W_PASSES * N], U32, name="w_codes", align_bytes=64)
+        w_scales = held.tile([P, W_PASSES * N], U8, name="w_scales", align_bytes=64)
+        results = held.tile([P, SLOTS], F32, name="results")
+        warm = held.tile([P, 1], F32, name="warm")
+
+        nc.vector.memset(warm[:], 0.0)
+        nc.scalar.activation(warm[:], warm[:], ACT.Gelu_apprx_tanh)
+        nc.gpsimd.memset(x_scales[:], 0)
+
+        w_rows = w.flatten_outer_dims().rearrange("(g p j) n -> p g (j n)", p=P, j=PACK)
+
+        loads = [("x", item) for item in range(len(X_CHUNKS))]
+        first = 0
+        w_groups = []
+        for count in W_LOADS:
+            loads.append(("w", len(w_groups)))
+            w_groups.append((first, count))
+            first += count
+        loads.extend([("gate", r) for r in range(TOP)])
+        raw = {}
+        issued = [0]
+
+        def load_until(limit):
+            while issued[0] < min(limit, len(loads)):
+                kind, item = loads[issued[0]]
+                tile = stream.tile([P, 2048], F32, name="raw")
+                raw[(kind, item)] = tile
+                if kind == "x":
+                    a, t0, width = X_CHUNKS[item]
+                    nc.sync.dma_start(
+                        out=tile[:, : PACK * width].rearrange("p (j t) -> p j t", j=PACK),
+                        in_=xT[a * K_PASS : (a + 1) * K_PASS, t0 : t0 + width].rearrange("(p j) t -> p j t", j=PACK),
+                    )
+                elif kind == "w":
+                    g0, count = w_groups[item]
+                    nc.sync.dma_start(
+                        out=tile[:, : count * PASS_COLS].rearrange("p (g c) -> p g c", g=count),
+                        in_=w_rows[:, g0 : g0 + count, :],
+                    )
+                else:
+                    nc.sync.dma_start(out=tile[:, :T], in_=gate[item])
+                issued[0] += 1
+                if issued[0] == 3:
+                    nc.sync.dma_start(slot_list[:], offs)
+                if issued[0] == BIAS_AFTER:
+                    nc.sync.dma_start(out=bias[:], in_=b)
+                    for place_list, pos in zip(place_lists, (pos1, pos2, pos3)):
+                        nc.sync.dma_start(place_list[:], pos)
+
+        def round_copy(on_vector, dst, values):
+            if on_vector:
+                nc.vector.tensor_copy(out=dst, in_=values)
+            else:
+                nc.scalar.copy(out=dst, in_=values)
+
+        x_grouped = {}
+
+        def round_x(item):
+            a, t0, width = X_CHUNKS[item]
+            grouped = x_stage.tile([P, 2048], BF16, name="grouped", align_bytes=64)
+            x_grouped[item] = grouped
+            round_copy(
+                item in VECTOR_X,
+                grouped[:, : PACK * width].rearrange("p (c i j) -> p c j i", i=4, j=PACK),
+                raw[("x", item)][:, : PACK * width].rearrange("p (j c i) -> p c j i", i=4, j=PACK),
+            )
+
+        def quantise_x(item):
+            a, t0, width = X_CHUNKS[item]
+            nc.vector.quantize_mx(
+                out=x_codes[a][:, t0 : t0 + width].bitcast(FP8X4),
+                scales=x_scales[4 * a : P, t0 : t0 + width],
+                in_=x_grouped[item][:, : PACK * width],
+            )
+
+        slot_codes = {}
+        slot_scales = {}
+
+        def gather(what, s):
+            s0, count = SLICES[s]
+            picks = slot_list[:, s0 // 16 : (s0 + count) // 16]
+            if what == "scales":
+                scales = slots_pool.tile([P, 512], U8, name="slot_scales_tile", align_bytes=64)
+                slot_scales[s] = scales
+                nc.vector.tensor_copy(scales[:, :count], x_scales[:].indirect(picks))
+            else:
+                codes = slots_pool.tile([P, 512], U32, name=f"slot_codes_tile{what}", align_bytes=64)
+                slot_codes[(what, s)] = codes
+                nc.vector.tensor_copy(codes[:, :count], x_codes[what][:].indirect(picks))
+
+        units = []
+        for group, (g0, count) in enumerate(w_groups):
+            for q in range(0, count, 2):
+                units.append((group, g0 + q, q, min(2, count - q)))
+        w_grouped = {}
+
+        def round_w(u):
+            group, g, q, n = units[u]
+            if q == 0:
+                grouped = w_stage.tile([P, 4 * PASS_COLS], BF16, name="w_grouped_tile", align_bytes=64)
+                w_grouped[group] = grouped
+            round_copy(
+                u in VECTOR_W,
+                w_grouped[group][:, q * PASS_COLS : (q + n) * PASS_COLS].rearrange("p (g c i j) -> p g c j i", c=N // 4, i=4, j=PACK),
+                raw[("w", group)][:, q * PASS_COLS : (q + n) * PASS_COLS].rearrange(
+                    "p (g j c i) -> p g c j i", c=N // 4, i=4, j=PACK
+                ),
+            )
+
+        def quantise_w(group):
+            g, n = w_groups[group]
+            nc.vector.quantize_mx(
+                out=w_codes[:, g * N : (g + n) * N].bitcast(FP8X4),
+                scales=w_scales[:, g * N : (g + n) * N],
+                in_=w_grouped[group][:, : n * PASS_COLS],
+            )
+
+        accs = {}
+        banks = []
+
+        def multiply(e):
+            if e % 4 == 0:
+                bank = psum.tile([P, 4 * C], F32, name="bank")
+                banks.append(bank)
+            acc = banks[-1][:, e % 4 * C : (e % 4 + 1) * C]
+            accs[e] = acc
+            s = e * C // 512
+            slots = slice(e * C - SLICES[s][0], (e + 1) * C - SLICES[s][0])
+            for a in range(PASSES):
+                cols = slice((e * PASSES + a) * N, (e * PASSES + a + 1) * N)
+                nc.tensor.matmul_mx(
+                    out=acc,
+                    lhsT=w_codes[:, cols].bitcast(FP8X4),
+                    lhsT_scale=w_scales[:, cols],
+                    rhs=slot_codes[(a, s)][:, slots].bitcast(FP8X4),
+                    rhs_scale=slot_scales[s][4 * a : P, slots],
+                    start=(a == 0),
+                    stop=(a == PASSES - 1),
+                )
+
+        def finish(e):
+            nc.scalar.activation(
+                results[:, e * C : (e + 1) * C], accs[e], ACT.Gelu_apprx_tanh, bias=bias[:, e : e + 1]
+            )
+
+        nx = len(X_CHUNKS)
+        gathers = [(a, s) for a in (0, 1) for s in range(SLICE_BUFS)]
+        for s in range(SLICE_BUFS):
+            gathers.extend([(2, s), ("scales", s)])
+        for s in range(SLICE_BUFS, len(SLICES)):
+            gathers.extend([(0, s), (1, s), (2, s), ("scales", s)])
+        x_gathers = {3: 2, 4: 1, 5: 2, 6: 1}
+        w_gathers = {0: 1, 1: 2}
+        gathered = set()
+
+        def gather_some(count):
+            for what, s in gathers[len(gathered) : len(gathered) + count]:
+                if s < SLICE_BUFS or done[0] >= 4 * (s - SLICE_BUFS + 1):
+                    gather(what, s)
+                    gathered.add((what, s))
+
+        done = [0]
+        finished = [0]
+        multiplied_at = {}
+        load_until(LOADS_AHEAD)
+        for item in range(nx):
+            load_until(item + 1 + LOADS_AHEAD)
+            round_x(item)
+            if item:
+                quantise_x(item - 1)
+            gather_some(x_gathers.get(item, 0))
+        passes_ready = 0
+        for u in range(len(units) + 1):
+            if u < len(units):
+                load_until(nx + units[u][0] + 1 + LOADS_AHEAD)
+                round_w(u)
+            if u == 0:
+                quantise_x(nx - 1)
+            else:
+                group, g, q, n = units[u - 1]
+                if q + n == w_groups[group][1]:
+                    quantise_w(group)
+                    passes_ready = g + n
+                while done[0] < E and (done[0] + 1) * PASSES <= passes_ready and ("scales", done[0] // 4) in gathered:
+                    multiply(done[0])
+                    multiplied_at[done[0]] = u
+                    done[0] += 1
+                while finished[0] < done[0] and multiplied_at[finished[0]] + GELU_LAG <= u:
+                    finish(finished[0])
+                    finished[0] += 1
+            gather_some(w_gathers.get(u, 1))
+        while finished[0] < E:
+            finish(finished[0])
+            finished[0] += 1
+
+        for t0, width in COMBINE:
+            cols = slice(t0, t0 + width)
+            terms = []
+            for r in range(TOP):
+                term = ends.tile([P, 512], F32, name=f"term{r}")
+                nc.vector.tensor_tensor(
+                    term[:, :width],
+                    results[:].indirect(place_lists[r][:, t0 // 16 : (t0 + width) // 16]),
+                    raw[("gate", r)][:, cols],
+                    ALU.mult,
+                )
+                terms.append(term)
+            part = ends.tile([P, 512], F32, name="part")
+            total = ends.tile([P, 512], F32, name="total")
+            nc.vector.tensor_tensor(part[:, :width], terms[0][:, :width], terms[1][:, :width], ALU.add)
+            nc.vector.tensor_tensor(total[:, :width], part[:, :width], terms[2][:, :width], ALU.add)
+            nc.sync.dma_start(out=out[:, cols], in_=total[:, :width])

@@ -23,15 +23,18 @@ SLOTS = E * C
 W_PASSES = E * PASSES
 PASS_COLS = PACK * N
 
-X_CHUNKS = ((0, 0, 128), (0, 128, 128), (0, 256, 512), (1, 0, 512), (1, 512, 256), (2, 0, 512), (2, 512, 256))
+X_CHUNKS = ((0, 0, 128), (0, 128, 128), (0, 256, 256), (0, 512, 256), (1, 0, 512), (1, 512, 256), (2, 0, 512), (2, 512, 256))
 W_LOADS = [4] * 12 + [2, 2, 1, 1]
-LOADS_AHEAD = 10
-SLICES = ((0, 512), (512, 512), (1024, 512), (1536, 512), (2048, 256))
-SLICE_BUFS = 3
-VECTOR_X = (1, 6)
-BIAS_AFTER = 14
-VECTOR_W = (17, 20, 22, 25, 26, 27)
-GELU_LAG = 7
+LOADS_AHEAD = 8
+SLICE = 576
+SLICES = SLOTS // SLICE
+X_GATHERS = (0, 0, 0, 0, 2, 2, 1, 1)
+W_GATHERS = (0, 0, 3, 0, 0, 0, 0, 0, 0, 0, 1, 3, 0, 0, 3, 0, 1)
+VECTOR_X = (0, 2, 3)
+BIAS_AFTER = 17
+VECTOR_W = (14, 21, 23, 24, 26, 27)
+GPSIMD_W = ()
+GELU_LAG = 11
 COMBINE = ((0, 512), (512, 256))
 
 
@@ -39,10 +42,9 @@ def tile_moe_tk_lin_gelu_kernel(tc, xT, w, b, gate, offs, pos1, pos2, pos3, out)
     nc = tc.nc
     with ExitStack() as ctx:
         held = ctx.enter_context(tc.tile_pool(name="held", bufs=1))
-        stream = ctx.enter_context(tc.tile_pool(name="stream", bufs=12))
+        stream = ctx.enter_context(tc.tile_pool(name="stream", bufs=10))
         x_stage = ctx.enter_context(tc.tile_pool(name="x_stage", bufs=3))
-        w_stage = ctx.enter_context(tc.tile_pool(name="w_stage", bufs=6))
-        slots_pool = ctx.enter_context(tc.tile_pool(name="slots_pool", bufs=SLICE_BUFS))
+        w_stage = ctx.enter_context(tc.tile_pool(name="w_stage", bufs=10))
         ends = ctx.enter_context(tc.tile_pool(name="ends", bufs=1))
         psum = ctx.enter_context(tc.psum_pool(name="psum", bufs=8))
 
@@ -51,6 +53,8 @@ def tile_moe_tk_lin_gelu_kernel(tc, xT, w, b, gate, offs, pos1, pos2, pos3, out)
         bias = held.tile([P, E], F32, name="bias")
         x_codes = [held.tile([P, T], U32, name=f"x_codes{a}", align_bytes=64) for a in range(PASSES)]
         x_scales = held.tile([P, T], U8, name="x_scales", align_bytes=64)
+        slot_codes = [held.tile([P, SLOTS], U32, name=f"slot_codes{a}", align_bytes=64) for a in range(PASSES)]
+        slot_scales = held.tile([P, SLOTS], U8, name="slot_scales", align_bytes=64)
         w_codes = held.tile([P, W_PASSES * N], U32, name="w_codes", align_bytes=64)
         w_scales = held.tile([P, W_PASSES * N], U8, name="w_scales", align_bytes=64)
         results = held.tile([P, SLOTS], F32, name="results")
@@ -100,9 +104,13 @@ def tile_moe_tk_lin_gelu_kernel(tc, xT, w, b, gate, offs, pos1, pos2, pos3, out)
                     for place_list, pos in zip(place_lists, (pos1, pos2, pos3)):
                         nc.sync.dma_start(place_list[:], pos)
 
-        def round_copy(on_vector, dst, values):
-            if on_vector:
+        def round_copy(engine, dst, values):
+            if engine == "vector":
                 nc.vector.tensor_copy(out=dst, in_=values)
+            elif engine == "gpsimd":
+                nc.gpsimd.tensor_scalar(
+                    out=dst, in0=values, scalar1=1.0, scalar2=0.0, op0=ALU.mult, op1=ALU.add
+                )
             else:
                 nc.scalar.copy(out=dst, in_=values)
 
@@ -113,7 +121,7 @@ def tile_moe_tk_lin_gelu_kernel(tc, xT, w, b, gate, offs, pos1, pos2, pos3, out)
             grouped = x_stage.tile([P, 2048], BF16, name="grouped", align_bytes=64)
             x_grouped[item] = grouped
             round_copy(
-                item in VECTOR_X,
+                "vector" if item in VECTOR_X else "scalar",
                 grouped[:, : PACK * width].rearrange("p (c i j) -> p c j i", i=4, j=PACK),
                 raw[("x", item)][:, : PACK * width].rearrange("p (j c i) -> p c j i", i=4, j=PACK),
             )
@@ -126,20 +134,13 @@ def tile_moe_tk_lin_gelu_kernel(tc, xT, w, b, gate, offs, pos1, pos2, pos3, out)
                 in_=x_grouped[item][:, : PACK * width],
             )
 
-        slot_codes = {}
-        slot_scales = {}
-
         def gather(what, s):
-            s0, count = SLICES[s]
-            picks = slot_list[:, s0 // 16 : (s0 + count) // 16]
+            picks = slot_list[:, s * (SLICE // 16) : (s + 1) * (SLICE // 16)]
+            cols = slice(s * SLICE, (s + 1) * SLICE)
             if what == "scales":
-                scales = slots_pool.tile([P, 512], U8, name="slot_scales_tile", align_bytes=64)
-                slot_scales[s] = scales
-                nc.vector.tensor_copy(scales[:, :count], x_scales[:].indirect(picks))
+                nc.vector.tensor_copy(slot_scales[:, cols], x_scales[:].indirect(picks))
             else:
-                codes = slots_pool.tile([P, 512], U32, name=f"slot_codes_tile{what}", align_bytes=64)
-                slot_codes[(what, s)] = codes
-                nc.vector.tensor_copy(codes[:, :count], x_codes[what][:].indirect(picks))
+                nc.vector.tensor_copy(slot_codes[what][:, cols], x_codes[what][:].indirect(picks))
 
         units = []
         for group, (g0, count) in enumerate(w_groups):
@@ -153,7 +154,7 @@ def tile_moe_tk_lin_gelu_kernel(tc, xT, w, b, gate, offs, pos1, pos2, pos3, out)
                 grouped = w_stage.tile([P, 4 * PASS_COLS], BF16, name="w_grouped_tile", align_bytes=64)
                 w_grouped[group] = grouped
             round_copy(
-                u in VECTOR_W,
+                "vector" if u in VECTOR_W else "gpsimd" if u in GPSIMD_W else "scalar",
                 w_grouped[group][:, q * PASS_COLS : (q + n) * PASS_COLS].rearrange("p (g c i j) -> p g c j i", c=N // 4, i=4, j=PACK),
                 raw[("w", group)][:, q * PASS_COLS : (q + n) * PASS_COLS].rearrange(
                     "p (g j c i) -> p g c j i", c=N // 4, i=4, j=PACK
@@ -177,16 +178,15 @@ def tile_moe_tk_lin_gelu_kernel(tc, xT, w, b, gate, offs, pos1, pos2, pos3, out)
                 banks.append(bank)
             acc = banks[-1][:, e % 4 * C : (e % 4 + 1) * C]
             accs[e] = acc
-            s = e * C // 512
-            slots = slice(e * C - SLICES[s][0], (e + 1) * C - SLICES[s][0])
+            slots = slice(e * C, (e + 1) * C)
             for a in range(PASSES):
                 cols = slice((e * PASSES + a) * N, (e * PASSES + a + 1) * N)
                 nc.tensor.matmul_mx(
                     out=acc,
                     lhsT=w_codes[:, cols].bitcast(FP8X4),
                     lhsT_scale=w_scales[:, cols],
-                    rhs=slot_codes[(a, s)][:, slots].bitcast(FP8X4),
-                    rhs_scale=slot_scales[s][4 * a : P, slots],
+                    rhs=slot_codes[a][:, slots].bitcast(FP8X4),
+                    rhs_scale=slot_scales[4 * a : P, slots],
                     start=(a == 0),
                     stop=(a == PASSES - 1),
                 )
@@ -197,20 +197,15 @@ def tile_moe_tk_lin_gelu_kernel(tc, xT, w, b, gate, offs, pos1, pos2, pos3, out)
             )
 
         nx = len(X_CHUNKS)
-        gathers = [(a, s) for a in (0, 1) for s in range(SLICE_BUFS)]
-        for s in range(SLICE_BUFS):
+        gathers = [(a, s) for a in (0, 1) for s in range(SLICES)]
+        for s in range(SLICES):
             gathers.extend([(2, s), ("scales", s)])
-        for s in range(SLICE_BUFS, len(SLICES)):
-            gathers.extend([(0, s), (1, s), (2, s), ("scales", s)])
-        x_gathers = {3: 2, 4: 1, 5: 2, 6: 1}
-        w_gathers = {0: 1, 1: 2}
         gathered = set()
 
         def gather_some(count):
             for what, s in gathers[len(gathered) : len(gathered) + count]:
-                if s < SLICE_BUFS or done[0] >= 4 * (s - SLICE_BUFS + 1):
-                    gather(what, s)
-                    gathered.add((what, s))
+                gather(what, s)
+                gathered.add((what, s))
 
         done = [0]
         finished = [0]
@@ -221,7 +216,7 @@ def tile_moe_tk_lin_gelu_kernel(tc, xT, w, b, gate, offs, pos1, pos2, pos3, out)
             round_x(item)
             if item:
                 quantise_x(item - 1)
-            gather_some(x_gathers.get(item, 0))
+            gather_some(X_GATHERS[item])
         passes_ready = 0
         for u in range(len(units) + 1):
             if u < len(units):
@@ -234,14 +229,14 @@ def tile_moe_tk_lin_gelu_kernel(tc, xT, w, b, gate, offs, pos1, pos2, pos3, out)
                 if q + n == w_groups[group][1]:
                     quantise_w(group)
                     passes_ready = g + n
-                while done[0] < E and (done[0] + 1) * PASSES <= passes_ready and ("scales", done[0] // 4) in gathered:
+                while done[0] < E and (done[0] + 1) * PASSES <= passes_ready and ("scales", ((done[0] + 1) * C - 1) // SLICE) in gathered:
                     multiply(done[0])
                     multiplied_at[done[0]] = u
                     done[0] += 1
                 while finished[0] < done[0] and multiplied_at[finished[0]] + GELU_LAG <= u:
                     finish(finished[0])
                     finished[0] += 1
-            gather_some(w_gathers.get(u, 1))
+            gather_some(W_GATHERS[u] if u < len(W_GATHERS) else len(gathers))
         while finished[0] < E:
             finish(finished[0])
             finished[0] += 1

@@ -29,12 +29,13 @@ LOADS_AHEAD = 8
 SLICE = 576
 SLICES = SLOTS // SLICE
 X_GATHERS = (0, 0, 0, 0, 2, 2, 1, 1)
-W_GATHERS = (0, 0, 3, 0, 0, 0, 0, 0, 0, 0, 1, 3, 0, 0, 3, 0, 1)
-VECTOR_X = (0, 2, 3)
-BIAS_AFTER = 17
-VECTOR_W = (14, 21, 23, 24, 26, 27)
+W_GATHERS = (0, 0, 0, 0, 0, 0, 0, 0, 1, 0, 0, 3, 1, 0, 1, 2, 3)
+VECTOR_X = (0, 1, 2, 3)
+BIAS_LOADS = ((24, 0, 18),)
+LISTS_AFTER = 16
+VECTOR_W = (22, 24, 26)
 GPSIMD_W = ()
-GELU_LAG = 11
+GELU_LAG = 10
 COMBINE = ((0, 512), (512, 256))
 
 
@@ -99,18 +100,16 @@ def tile_moe_tk_lin_gelu_kernel(tc, xT, w, b, gate, offs, pos1, pos2, pos3, out)
                 issued[0] += 1
                 if issued[0] == 3:
                     nc.sync.dma_start(slot_list[:], offs)
-                if issued[0] == BIAS_AFTER:
-                    nc.sync.dma_start(out=bias[:], in_=b)
+                for after, e0, e1 in BIAS_LOADS:
+                    if issued[0] == after:
+                        nc.sync.dma_start(out=bias[:, e0:e1], in_=b[:, e0:e1])
+                if issued[0] == LISTS_AFTER:
                     for place_list, pos in zip(place_lists, (pos1, pos2, pos3)):
                         nc.sync.dma_start(place_list[:], pos)
 
         def round_copy(engine, dst, values):
             if engine == "vector":
                 nc.vector.tensor_copy(out=dst, in_=values)
-            elif engine == "gpsimd":
-                nc.gpsimd.tensor_scalar(
-                    out=dst, in0=values, scalar1=1.0, scalar2=0.0, op0=ALU.mult, op1=ALU.add
-                )
             else:
                 nc.scalar.copy(out=dst, in_=values)
 
@@ -153,8 +152,23 @@ def tile_moe_tk_lin_gelu_kernel(tc, xT, w, b, gate, offs, pos1, pos2, pos3, out)
             if q == 0:
                 grouped = w_stage.tile([P, 4 * PASS_COLS], BF16, name="w_grouped_tile", align_bytes=64)
                 w_grouped[group] = grouped
+            if u in GPSIMD_W:
+                for h in range(q, q + n):
+                    nc.gpsimd.tensor_scalar(
+                        out=w_grouped[group][:, h * PASS_COLS : (h + 1) * PASS_COLS].rearrange(
+                            "p (c i j) -> p c j i", i=4, j=PACK
+                        ),
+                        in0=raw[("w", group)][:, h * PASS_COLS : (h + 1) * PASS_COLS].rearrange(
+                            "p (j c i) -> p c j i", i=4, j=PACK
+                        ),
+                        scalar1=1.0,
+                        scalar2=0.0,
+                        op0=ALU.mult,
+                        op1=ALU.add,
+                    )
+                return
             round_copy(
-                "vector" if u in VECTOR_W else "gpsimd" if u in GPSIMD_W else "scalar",
+                "vector" if u in VECTOR_W else "scalar",
                 w_grouped[group][:, q * PASS_COLS : (q + n) * PASS_COLS].rearrange("p (g c i j) -> p g c j i", c=N // 4, i=4, j=PACK),
                 raw[("w", group)][:, q * PASS_COLS : (q + n) * PASS_COLS].rearrange(
                     "p (g j c i) -> p g c j i", c=N // 4, i=4, j=PACK
@@ -241,20 +255,39 @@ def tile_moe_tk_lin_gelu_kernel(tc, xT, w, b, gate, offs, pos1, pos2, pos3, out)
             finish(finished[0])
             finished[0] += 1
 
-        for t0, width in COMBINE:
-            cols = slice(t0, t0 + width)
-            terms = []
-            for r in range(TOP):
-                term = ends.tile([P, 512], F32, name=f"term{r}")
-                nc.vector.tensor_tensor(
-                    term[:, :width],
-                    results[:].indirect(place_lists[r][:, t0 // 16 : (t0 + width) // 16]),
-                    raw[("gate", r)][:, cols],
-                    ALU.mult,
-                )
-                terms.append(term)
-            part = ends.tile([P, 512], F32, name="part")
-            total = ends.tile([P, 512], F32, name="total")
-            nc.vector.tensor_tensor(part[:, :width], terms[0][:, :width], terms[1][:, :width], ALU.add)
-            nc.vector.tensor_tensor(total[:, :width], part[:, :width], terms[2][:, :width], ALU.add)
-            nc.sync.dma_start(out=out[:, cols], in_=total[:, :width])
+        terms = {}
+        parts = {}
+        totals = {}
+
+        def weigh(piece, r):
+            t0, width = COMBINE[piece]
+            term = ends.tile([P, width], F32, name=f"term{piece}{r}")
+            terms[(piece, r)] = term
+            nc.vector.tensor_tensor(
+                term[:],
+                results[:].indirect(place_lists[r][:, t0 // 16 : (t0 + width) // 16]),
+                raw[("gate", r)][:, t0 : t0 + width],
+                ALU.mult,
+            )
+
+        def add_two(piece):
+            part = ends.tile([P, COMBINE[piece][1]], F32, name=f"part{piece}")
+            parts[piece] = part
+            nc.vector.tensor_tensor(part[:], terms[(piece, 0)][:], terms[(piece, 1)][:], ALU.add)
+
+        def add_third(piece):
+            t0, width = COMBINE[piece]
+            total = ends.tile([P, width], F32, name=f"total{piece}")
+            nc.vector.tensor_tensor(total[:], parts[piece][:], terms[(piece, 2)][:], ALU.add)
+            nc.sync.dma_start(out=out[:, t0 : t0 + width], in_=total[:])
+
+        weigh(0, 0)
+        weigh(0, 1)
+        weigh(1, 0)
+        add_two(0)
+        weigh(0, 2)
+        weigh(1, 1)
+        weigh(1, 2)
+        add_two(1)
+        add_third(0)
+        add_third(1)

from contextlib import ExitStack

import concourse.mybir as mybir

K, T, E, C, N = 1536, 768, 18, 128, 128
TOP = 3
FLOPS = 2 * K * N * TOP * T

F32 = mybir.dt.float32
BF16 = mybir.dt.bfloat16
U32 = mybir.dt.uint32
U16 = mybir.dt.uint16
U8 = mybir.dt.uint8
FP8X4 = mybir.dt.float8_e4m3fn_x4
ACT = mybir.ActivationFunctionType
ALU = mybir.AluOpType

P = 128
PACK = 4
K_PASS = P * PACK
PASSES = K // K_PASS
SLOTS = E * C
W_PASSES = E * PASSES
PASS_COLS = PACK * N

X_CHUNKS = ((0, 0, 128), (0, 128, 128), (0, 256, 256), (0, 512, 256), (1, 0, 512), (1, 512, 256), (2, 0, 512), (2, 512, 256))
W_LOADS = [4] * 12 + [2, 2, 1, 1]
LOADS_AHEAD = 8
SLICE = 576
SLICES = SLOTS // SLICE
X_GATHERS = (0, 0, 0, 0, 2, 2, 1, 1)
W_GATHERS = (0, 0, 0, 0, 0, 0, 0, 0, 1, 0, 0, 3, 1, 0, 1, 2, 3)
VECTOR_X = (0, 1, 2, 3)
BIAS_LOADS = ((24, 0, 18),)
LISTS_AFTER = 16
VECTOR_W = (22, 24, 26)
GPSIMD_W = ()
GELU_LAG = 10
COMBINE = ((0, 512), (512, 256))


def tile_moe_tk_lin_gelu_kernel(tc, xT, w, b, gate, offs, pos1, pos2, pos3, out):
    nc = tc.nc
    with ExitStack() as ctx:
        held = ctx.enter_context(tc.tile_pool(name="held", bufs=1))
        stream = ctx.enter_context(tc.tile_pool(name="stream", bufs=10))
        x_stage = ctx.enter_context(tc.tile_pool(name="x_stage", bufs=3))
        w_stage = ctx.enter_context(tc.tile_pool(name="w_stage", bufs=10))
        ends = ctx.enter_context(tc.tile_pool(name="ends", bufs=1))
        psum = ctx.enter_context(tc.psum_pool(name="psum", bufs=8))

        slot_list = held.tile([P, SLOTS // 16], U16, name="slot_list")
        place_lists = [held.tile([P, T // 16], U16, name=f"place_list{r}") for r in range(TOP)]
        bias = held.tile([P, E], F32, name="bias")
        x_codes = [held.tile([P, T], U32, name=f"x_codes{a}", align_bytes=64) for a in range(PASSES)]
        x_scales = held.tile([P, T], U8, name="x_scales", align_bytes=64)
        slot_codes = [held.tile([P, SLOTS], U32, name=f"slot_codes{a}", align_bytes=64) for a in range(PASSES)]
        slot_scales = held.tile([P, SLOTS], U8, name="slot_scales", align_bytes=64)
        w_codes = held.tile([P, W_PASSES * N], U32, name="w_codes", align_bytes=64)
        w_scales = held.tile([P, W_PASSES * N], U8, name="w_scales", align_bytes=64)
        results = held.tile([P, SLOTS], F32, name="results")
        warm = held.tile([P, 1], F32, name="warm")

        nc.vector.memset(warm[:], 0.0)
        nc.scalar.activation(warm[:], warm[:], ACT.Gelu_apprx_tanh)
        nc.gpsimd.memset(x_scales[:], 0)

        w_rows = w.flatten_outer_dims().rearrange("(g p j) n -> p g (j n)", p=P, j=PACK)

        loads = [("x", item) for item in range(len(X_CHUNKS))]
        first = 0
        w_groups = []
        for count in W_LOADS:
            loads.append(("w", len(w_groups)))
            w_groups.append((first, count))
            first += count
        loads.extend([("gate", r) for r in range(TOP)])
        raw = {}
        issued = [0]

        def load_until(limit):
            while issued[0] < min(limit, len(loads)):
                kind, item = loads[issued[0]]
                tile = stream.tile([P, 2048], F32, name="raw")
                raw[(kind, item)] = tile
                if kind == "x":
                    a, t0, width = X_CHUNKS[item]
                    nc.sync.dma_start(
                        out=tile[:, : PACK * width].rearrange("p (j t) -> p j t", j=PACK),
                        in_=xT[a * K_PASS : (a + 1) * K_PASS, t0 : t0 + width].rearrange("(p j) t -> p j t", j=PACK),
                    )
                elif kind == "w":
                    g0, count = w_groups[item]
                    nc.sync.dma_start(
                        out=tile[:, : count * PASS_COLS].rearrange("p (g c) -> p g c", g=count),
                        in_=w_rows[:, g0 : g0 + count, :],
                    )
                else:
                    nc.sync.dma_start(out=tile[:, :T], in_=gate[item])
                issued[0] += 1
                if issued[0] == 3:
                    nc.sync.dma_start(slot_list[:], offs)
                for after, e0, e1 in BIAS_LOADS:
                    if issued[0] == after:
                        nc.sync.dma_start(out=bias[:, e0:e1], in_=b[:, e0:e1])
                if issued[0] == LISTS_AFTER:
                    for place_list, pos in zip(place_lists, (pos1, pos2, pos3)):
                        nc.sync.dma_start(place_list[:], pos)

        def round_copy(engine, dst, values):
            if engine == "vector":
                nc.vector.tensor_copy(out=dst, in_=values)
            else:
                nc.scalar.copy(out=dst, in_=values)

        x_grouped = {}

        def round_x(item):
            a, t0, width = X_CHUNKS[item]
            grouped = x_stage.tile([P, 2048], BF16, name="grouped", align_bytes=64)
            x_grouped[item] = grouped
            round_copy(
                "vector" if item in VECTOR_X else "scalar",
                grouped[:, : PACK * width].rearrange("p (c i j) -> p c j i", i=4, j=PACK),
                raw[("x", item)][:, : PACK * width].rearrange("p (j c i) -> p c j i", i=4, j=PACK),
            )

        def quantise_x(item):
            a, t0, width = X_CHUNKS[item]
            nc.vector.quantize_mx(
                out=x_codes[a][:, t0 : t0 + width].bitcast(FP8X4),
                scales=x_scales[4 * a : P, t0 : t0 + width],
                in_=x_grouped[item][:, : PACK * width],
            )

        def gather(what, s):
            picks = slot_list[:, s * (SLICE // 16) : (s + 1) * (SLICE // 16)]
            cols = slice(s * SLICE, (s + 1) * SLICE)
            if what == "scales":
                nc.vector.tensor_copy(slot_scales[:, cols], x_scales[:].indirect(picks))
            else:
                nc.vector.tensor_copy(slot_codes[what][:, cols], x_codes[what][:].indirect(picks))

        units = []
        for group, (g0, count) in enumerate(w_groups):
            for q in range(0, count, 2):
                units.append((group, g0 + q, q, min(2, count - q)))
        w_grouped = {}

        def round_w(u):
            group, g, q, n = units[u]
            if q == 0:
                grouped = w_stage.tile([P, 4 * PASS_COLS], BF16, name="w_grouped_tile", align_bytes=64)
                w_grouped[group] = grouped
            if u in GPSIMD_W:
                for h in range(q, q + n):
                    nc.gpsimd.tensor_scalar(
                        out=w_grouped[group][:, h * PASS_COLS : (h + 1) * PASS_COLS].rearrange(
                            "p (c i j) -> p c j i", i=4, j=PACK
                        ),
                        in0=raw[("w", group)][:, h * PASS_COLS : (h + 1) * PASS_COLS].rearrange(
                            "p (j c i) -> p c j i", i=4, j=PACK
                        ),
                        scalar1=1.0,
                        scalar2=0.0,
                        op0=ALU.mult,
                        op1=ALU.add,
                    )
                return
            round_copy(
                "vector" if u in VECTOR_W else "scalar",
                w_grouped[group][:, q * PASS_COLS : (q + n) * PASS_COLS].rearrange("p (g c i j) -> p g c j i", c=N // 4, i=4, j=PACK),
                raw[("w", group)][:, q * PASS_COLS : (q + n) * PASS_COLS].rearrange(
                    "p (g j c i) -> p g c j i", c=N // 4, i=4, j=PACK
                ),
            )

        def quantise_w(group):
            g, n = w_groups[group]
            nc.vector.quantize_mx(
                out=w_codes[:, g * N : (g + n) * N].bitcast(FP8X4),
                scales=w_scales[:, g * N : (g + n) * N],
                in_=w_grouped[group][:, : n * PASS_COLS],
            )

        accs = {}
        banks = []

        def multiply(e):
            if e % 4 == 0:
                bank = psum.tile([P, 4 * C], F32, name="bank")
                banks.append(bank)
            acc = banks[-1][:, e % 4 * C : (e % 4 + 1) * C]
            accs[e] = acc
            slots = slice(e * C, (e + 1) * C)
            for a in range(PASSES):
                cols = slice((e * PASSES + a) * N, (e * PASSES + a + 1) * N)
                nc.tensor.matmul_mx(
                    out=acc,
                    lhsT=w_codes[:, cols].bitcast(FP8X4),
                    lhsT_scale=w_scales[:, cols],
                    rhs=slot_codes[a][:, slots].bitcast(FP8X4),
                    rhs_scale=slot_scales[4 * a : P, slots],
                    start=(a == 0),
                    stop=(a == PASSES - 1),
                )

        def finish(e):
            nc.scalar.activation(
                results[:, e * C : (e + 1) * C], accs[e], ACT.Gelu_apprx_tanh, bias=bias[:, e : e + 1]
            )

        nx = len(X_CHUNKS)
        gathers = [(a, s) for a in (0, 1) for s in range(SLICES)]
        for s in range(SLICES):
            gathers.extend([(2, s), ("scales", s)])
        gathered = set()

        def gather_some(count):
            for what, s in gathers[len(gathered) : len(gathered) + count]:
                gather(what, s)
                gathered.add((what, s))

        done = [0]
        finished = [0]
        multiplied_at = {}
        load_until(LOADS_AHEAD)
        for item in range(nx):
            load_until(item + 1 + LOADS_AHEAD)
            round_x(item)
            if item:
                quantise_x(item - 1)
            gather_some(X_GATHERS[item])
        passes_ready = 0
        for u in range(len(units) + 1):
            if u < len(units):
                load_until(nx + units[u][0] + 1 + LOADS_AHEAD)
                round_w(u)
            if u == 0:
                quantise_x(nx - 1)
            else:
                group, g, q, n = units[u - 1]
                if q + n == w_groups[group][1]:
                    quantise_w(group)
                    passes_ready = g + n
                while done[0] < E and (done[0] + 1) * PASSES <= passes_ready and ("scales", ((done[0] + 1) * C - 1) // SLICE) in gathered:
                    multiply(done[0])
                    multiplied_at[done[0]] = u
                    done[0] += 1
                while finished[0] < done[0] and multiplied_at[finished[0]] + GELU_LAG <= u:
                    finish(finished[0])
                    finished[0] += 1
            gather_some(W_GATHERS[u] if u < len(W_GATHERS) else len(gathers))
        while finished[0] < E:
            finish(finished[0])
            finished[0] += 1

        terms = {}
        parts = {}
        totals = {}

        def weigh(piece, r):
            t0, width = COMBINE[piece]
            term = ends.tile([P, width], F32, name=f"term{piece}{r}")
            terms[(piece, r)] = term
            nc.vector.tensor_tensor(
                term[:],
                results[:].indirect(place_lists[r][:, t0 // 16 : (t0 + width) // 16]),
                raw[("gate", r)][:, t0 : t0 + width],
                ALU.mult,
            )

        def add_two(piece):
            part = ends.tile([P, COMBINE[piece][1]], F32, name=f"part{piece}")
            parts[piece] = part
            nc.vector.tensor_tensor(part[:], terms[(piece, 0)][:], terms[(piece, 1)][:], ALU.add)

        def add_third(piece):
            t0, width = COMBINE[piece]
            total = ends.tile([P, width], F32, name=f"total{piece}")
            nc.vector.tensor_tensor(total[:], parts[piece][:], terms[(piece, 2)][:], ALU.add)
            nc.sync.dma_start(out=out[:, t0 : t0 + width], in_=total[:])

        weigh(0, 0)
        weigh(0, 1)
        weigh(1, 0)
        add_two(0)
        weigh(0, 2)
        weigh(1, 1)
        weigh(1, 2)
        add_two(1)
        add_third(0)
        add_third(1)
